import numpy as np, ml_dtypes
CORES = [2,3,42,43,82,83,122,123]
N = 8
BF = ml_dtypes.bfloat16
def gentries(a):
    return np.ascontiguousarray(a.reshape(8, 16, -1).transpose(0, 2, 1)).reshape(8, -1)
def gtable(e):
    e = np.asarray(e); return np.ascontiguousarray(e.reshape(8, -1, 16).transpose(0, 2, 1)).reshape(128, -1).astype(np.int32)
W, K, E, X, S, RO = 8192, 3072, 128, 3, 3, 2
ANY = np.arange(256); LEN = np.arange(1, 13)
def place(u1, u2, m):
    return ((((u1 & 4095) * (u2 & 4095)) >> 5) + u2 + 97 * m) & (W - 1)
def hashes(st, m, wt):
    u = np.where(np.arange(12) < m[:, None], st, 0) @ wt
    return place(u[:, 0], u[:, 1], m)
def ropes(rng, shape, lens):
    n = np.minimum(rng.integers(0, 8, shape), 4)
    return np.where(np.arange(4) < n[..., None], lens[rng.integers(0, len(lens), shape + (4,))], 0)
def fill(rng):
    return np.concatenate([rng.integers(0, 256, (N, 8, 12, W)), np.moveaxis(ropes(rng, (N, 8, W), LEN), 3, 2)], axis=2)
def pool(rng, M, vals):
    st = vals[rng.integers(0, len(vals), (M, 12))]; h = max(M // 8, 1); keep = rng.integers(0, 13, M); keep[:h] = 0
    return np.where(np.arange(12) < keep[:, None], st[rng.integers(0, h, M)], st)
def plant(T, st, m, ro, wt):
    h = hashes(st, m, wt); T[:, h] = np.concatenate([st.T, ro.T])
def asks(rng, st, vals, lens):
    x = st[rng.integers(0, len(st), K)]; cut = np.where(rng.random(K) < 0.3, rng.integers(0, 13, K), 12)
    x = np.where(np.arange(12) < cut[:, None], x, vals[rng.integers(0, len(vals), (K, 12))])
    return np.concatenate([x.T, ropes(rng, (K,), lens).T])
def parts(rng, wt, M, n, vals, lens):
    P = fill(rng); q = np.zeros((N, 8, 16, K), np.int64)
    for g in range(8):
        st = pool(rng, int(M[g]), vals)
        for a in range(N):
            plant(P[a, g], st[rng.integers(0, len(st), n)], lens[rng.integers(0, len(lens), n)], ropes(rng, (n,), lens), wt[a, g])
            q[a, g] = asks(rng, st, vals, lens)
    return P, q
def alike_ropes(n, l):
    return np.tile(np.array((tuple(l) + (0, 0, 0, 0))[:4]), (n, 1))
def steer(rng, c):
    v = ((np.diff(c, axis=1, prepend=0) - 194) & (W - 1)) + W * rng.integers(0, 65280 // W, c.shape)
    return np.stack([v % 255, v // 255], axis=2).reshape(len(c), 12)
def meetings(rng, ends):
    n = 6; F = 2 + 2 * S; cut = 2 + n * np.arange(7); four = (6, 8, 10, 12)
    c = 1 + rng.permutation(W - 2)[:(2 + 7 * n) * 6].reshape(-1, 6)
    d, s1, e1, q2, s3, o3, q4, s5 = np.split(c, cut)
    for i in range(2): d[i, ends[i][0]] = ends[i][1]
    s1[:, 1] = s1[:, 0]; e1[:, 0] = s1[:, 0]
    q2[:, S] = q2[:, 1]
    s3[:, S - 1] = s3[:, S]; o3[:, :2] = s3[:, :2]
    q4[:, 3] = q4[:, 1]
    s5[:, 5] = s5[:, 2]
    x = steer(rng, c); d, s1, e1, q2, s3, o3, q4, s5 = np.split(x, cut)
    e1[:, :2] = s1[:, :2]; o3[:, :4] = s3[:, :4]
    r2 = q2.copy(); r2[:, 4:] = (r2[:, 4:] + rng.integers(1, 256, (n, 8))) & 255
    r4 = q4.copy(); r4[:, 4:] = (r4[:, 4:] + rng.integers(1, 256, (n, 8))) & 255
    marks = [(d, 4, four), (d, F + 2, ()), (s1, 4, four), (s1, F + 2, ()), (r2, 4, four), (q2, F + 2, ()), (s3, 4, four), (s3, F + 2, ()), (o3, F, ()), (r4, 4, ()), (s5, 4, (6,))]
    ask = [(d, (4,)), (s1, (4,)), (q2, (F,)), (s3, (4,)), (o3, (4,)), (q4, (8,)), (s5, (4,)), (s5, (12,)), (e1, (12, 2)), (q2, (4,)), (q4, (8, 4))]
    return marks, np.concatenate([y for y, l in ask]), np.concatenate([alike_ropes(len(y), l) for y, l in ask]), 2 + 7 * n
def pack(P, q, wt):
    w = np.concatenate([wt, np.zeros((N, 8, 4, 2), np.int64)], axis=2)
    return {"mk": P.reshape(N, 128, W).astype(np.float32).astype(BF), "qs": q.reshape(N, 128, K).astype(np.float32).astype(BF), "wt": w.reshape(N, 128, 2).astype(np.float32).astype(BF)}
def setup_inputs(rng):
    wt = rng.integers(0, 256, (N, 8, 12, 2)); P, q = parts(rng, wt, [512] * 8, 3 * W // 4, ANY, LEN)
    return pack(P, q, wt)
def setup_inputs_alike(rng):
    wt = rng.integers(0, 256, (N, 8, 12, 2)); P, q = parts(rng, wt, rng.integers(16, 33, 8), 160, ANY, LEN)
    return pack(P, q, wt)
def setup_inputs_ends(rng):
    wt = rng.choice(np.array([0, 1, 255]), (N, 8, 12, 2)); wt[:, 3] = 0; wt[:, 5] = 255
    for g in (0, 1, 6):
        wt[:, g] = 0; wt[:, g, 0::2, 1] = 1; wt[:, g, 1::2, 1] = 255
    P, q = parts(rng, wt, [64] * 8, W // 4, np.array([0, 255, 0, 1, 254]), np.array([1, 12, 1, 12, 2, 11]))
    for g, ends in ((0, ((S, 0), (1, W - 1))), (1, ((S + 1, 0), (S + 1, W - 1))), (6, ((S, W - 1), (1, 0)))):
        marks, st, ro, look = meetings(rng, ends)
        for a in range(N):
            for y, m, l in marks: plant(P[a, g], y, np.full(len(y), m), alike_ropes(len(y), l), wt[a, g])
            j = np.concatenate([rng.permutation(len(st)), rng.integers(0, look, K - len(st))])
            q[a, g] = np.concatenate([st[j].T, ro[j].T])
    x = rng.integers(225, 256, (2048, 12)); x = x[np.unique(np.sum(x, axis=1), return_index=True)[1]]
    u = 255 * np.sum(x, axis=1); x = x[np.argsort(-((((u & 4095) ** 2) >> 5) + u))[:24]]
    for a in range(N):
        plant(P[a, 5], x, np.full(len(x), 12), np.zeros((len(x), 4), np.int64), wt[a, 5])
        t = rng.permutation(K)[:96]; q[a, 5][:12, t] = x[np.arange(96) % len(x)].T; q[a, 5][12:, t] = np.array([12, 0, 0, 0])[:, None]
    return pack(P, q, wt)
def setup_inputs_full(rng):
    w = rng.integers(0, 256, (8, 12, 2)); wt = np.stack([w] * N); P = fill(rng); q = np.zeros((N, 8, 16, K), np.int64)
    for g in range(8):
        st = rng.integers(0, 256, (2048, 12)); hs = np.stack([hashes(st, np.full(2048, m), w[g]) for m in [5] + [9 + i for i in range(S)]])
        used = set(); keep = []
        for i in range(2048):
            c = set(hs[:, i].tolist())
            if len(keep) < E and len(c) == S + 1 and not (c & used):
                used |= c; keep.append(i)
        x = st[np.array(keep)]; n = len(keep)
        for a in range(N):
            plant(P[a, g], x, np.full(n, 5), np.stack([np.array([9, 10, 11, 12])] * n), w[g])
            plant(P[a, g], x, np.full(n, 8 + S), np.zeros((n, 4), np.int64), w[g])
            j = np.concatenate([rng.permutation(n), rng.integers(0, n, K - n)])
            first = (rng.random(K) < 0.5) | (np.arange(K) < n)
            ro = np.where(first[:, None], np.array([5, 8, 0, 0]), np.array([7 + S, 5, 12, 0]))
            q[a, g] = np.concatenate([x[j].T, ro.T])
    return pack(P, q, wt)
def setup_inputs_still(rng):
    wt = rng.integers(0, 256, (N, 8, 12, 2)); P, q = parts(rng, wt, [256] * 8, W // 2, ANY, LEN); e = rng.permutation(8)
    q[:, :, 12:] = np.where(rng.random((N, 8, 1, K)) < 0.5, 0, q[:, :, 12:])
    q[:, e[0], 12:] = 0; P[:, e[1], 12:] = 0; q[:, e[2], :12] = rng.integers(0, 256, (N, 12, K))
    q[:, e[2], 12:] = np.where(q[:, e[2], 12:] > 0, np.maximum(q[:, e[2], 12:], 4), 0)
    return pack(P, q, wt)
def setup_inputs_spread(rng):
    vals = np.minimum(np.exp2(8.01 * rng.random(512)).astype(np.int64), 256) - 1
    wt = vals[rng.integers(0, 512, (N, 8, 12, 2))]; P, q = parts(rng, wt, 2 ** rng.integers(3, 12, 8), W // 2, vals, LEN)
    return pack(P, q, wt)
def check_inputs(d):
    bad = []
    for k, n in (("mk", W), ("qs", K), ("wt", 2)):
        v = np.asarray(d[k]).astype(np.float32).reshape(N, 8, 16, n)
        if not np.all(v == np.floor(v)): bad.append("whole numbers of " + k)
        if not (np.min(v) >= 0 and np.max(v[:, :, :12]) <= 255): bad.append("range of " + k)
        if not np.max(v[:, :, 12:]) <= (0 if k == "wt" else 12): bad.append("last four rows of " + k)
        if k != "wt" and np.any((v[:, :, 12:15] == 0) & (v[:, :, 13:] > 0)): bad.append("ropes of " + k)
    return bad
def reference(mk, qs, wt):
    P = mk.astype(np.float32).astype(np.int32).reshape(N, 8, 16, W); q = qs.astype(np.float32).astype(np.int32).reshape(N, 8, 16, K)
    w = np.ascontiguousarray(wt.astype(np.float32).astype(np.int32).reshape(N, 8, 16, 2)[:, :, :12].transpose(0, 1, 3, 2))
    p = np.arange(12, dtype=np.int32)[:, None]
    for rnd in range(RO):
        sy = q[:, :, :12]; ro = q[:, :, 12:]
        b = np.full((N, 8, K), -1, np.int32); f = np.full((N, 8, K), -1, np.int32); mb = np.zeros((N, 8, K), np.int32); mf = np.zeros((N, 8, K), np.int32)
        for step in range(S):
            m = ro[:, :, 0]
            u = np.matmul(w, np.where(p < m[:, :, None], sy, 0))
            h = place(u[:, :, 0], u[:, :, 1], m)
            v = np.take_along_axis(P, h[:, :, None], axis=3)
            same = np.all((v[:, :, :12] == sy) | (p >= m[:, :, None]), axis=2)
            hit = (m > 0) & same; miss = (m > 0) & ~same
            b = np.where(hit, h, b); mb = np.where(hit, m, mb)
            f = np.where(miss, h, np.where(hit, -1, f)); mf = np.where(miss, m, mf)
            less = np.concatenate([ro[:, :, 1:], np.zeros((N, 8, 1, K), np.int32)], axis=2)
            ro = np.where(hit[:, :, None], v[:, :, 12:], np.where(miss[:, :, None], less, ro))
        old = np.take_along_axis(P, np.maximum(b, 0)[:, :, None], axis=3)[:, :, :12]
        new = q.copy(); new[:, :, :12] = np.where((b >= 0)[:, :, None] & (p < mb[:, :, None] + X), old, sy)
        if rnd < RO - 1:
            for a in range(N):
                for g in range(8):
                    T = P[a, g]; c = np.nonzero((b[a, g, :E] >= 0) & (f[a, g, :E] >= 0))[0]
                    t = c[np.unique(f[a, g, c], return_index=True)[1]]
                    T[:, f[a, g, t]] = np.concatenate([sy[a, g][:, t], ro[a, g][:, t]])
                    t = c[np.unique(b[a, g, c], return_index=True)[1]]
                    have = T[12:15, b[a, g, t]]
                    T[12:, b[a, g, t]] = np.concatenate([mf[a, g, t][None], have])
            q = np.ascontiguousarray(new.reshape(N, 8, 16, N, K // N).transpose(3, 1, 2, 0, 4)).reshape(N, 8, 16, K)
    return {"yq": new.reshape(N, 128, K).astype(np.float32).astype(BF), "yb": np.stack([gtable(x) for x in b]).astype(np.float32)}

@@ -1,0 +1,530 @@
+from concourse.bass import DstId, RemoteDMATransfer
+from concourse.mybir import AluOpType, AxisListType, ActivationFunctionType
+
+A = AluOpType
+F = ActivationFunctionType
+W, NC, CH, NN, S = 8192, 3, 1024, 64, 3
+BIG, SL = 2.0 ** 60, 7.6
+
+SCRATCH, BANKS = {}, []
+
+
+def _b(dtype, where, spec, k=1):
+    for x in spec.split():
+        n, w = x.split(":")
+        SCRATCH[n] = (where, [128, k * int(w)], dtype)
+        if where == "psum":
+            BANKS.append(n)
+
+
+_b("bfloat16", "sbuf", "mk0:8192 mk1:8320 wts:2 ones:132 idw:132 ident:128 nident:128 isym:128 sh1:128 sh2:128 spl:128 spa:128 "
+   "z8a:8 z8:8 bm:143 WX:143 WY:143 WE:143 WR0:143 WR1:143 WR2:143 thv:64 ths:64 tha:64 thb:64 th3:64 sel1:16 sel2:16 "
+   "mt:16 g0:128 ga1:128 ga2:128 wnew:128 g1:128 mfw:128 snew:128")
+_b("int32", "sbuf", "ip:1 i16:1 kai:8 fi:8 mfi:8 sbi:8")
+_b("uint16", "sbuf", "flu:16 tgu:16 sbl:8 mfl:8")
+_b("float32", "sbuf", "icol:1 m12:1 sil:1 wc:1 c12:1 c13:1 c14:1 ge13:1 ge14:1 mid:1 wcm:1 wtf:2 mrow:64 iot:8208 trow:256 "
+   "t16a:16 t16:16 dump16:16 act:24 ka:24 kam:8 ed1:8 ed0:8 ed:16 fbm:16 fbe:16 nb:16 krow:256 dk:2048 first:16 win:16 "
+   "gg:16 tgt:16")
+SCRATCH["yby"] = ("sbuf", [128, 8, 24], "float32")
+_b("bfloat16", "sbuf", "qa:1024 qb:1024 rr:1024 zz:1024 dd:1024 ld:1024 lm:1024 nwa:1024 nwb:1024", NC)
+_b("float32", "sbuf", "rq:192 xx:128 x2:64 n2:64 m2:64 m3:64 thr0:64 thr:64 w97:64 hit:64 kb:64 ybx:64", NC)
+_b("int32", "sbuf", "ui:128 ac:128 pp:64 kk:64 ss:64 hi:64 ki:64 bi:64 mbi:64", NC)
+_b("uint16", "sbuf", "ml:64 hl:64 bl:64 mbl:64", NC)
+_b("float32", "psum", "pn0:512 pn1:512 pn2:512 pw0:512 pw1:512 pw2:512 vp:512 pe:512")
+
+SEMAPHORES = ["sT", "sV", "sS", "sG", "lw", "lm0", "lm1", "lyb"]
+for _c in range(NC):
+    SEMAPHORES += ["lq%d" % _c, "slf%d" % _c, "arr%d" % _c, "snt%d" % _c, "out%d" % _c]
+
+VC, PC, VG, VGS, OV, WAKE = 1.0, 0.5, 1.5, 1.5, 20.0, 60.0
+BIAS = [91000.0, 6000.0, 92000.0, -297000.0, 0.0, 10000.0, 3000.0, 3000.0]
+Z_V = {(0, 0, 1), (0, 0, 2), (0, 1, 0), (0, 2, 0), (0, 2, 1), (1, 0, 0), (1, 0, 2), (1, 1, 0), (1, 1, 1), (1, 1, 2), (1, 2, 0)}
+D_S = {(1, 0, 1)}
+L_S = {(1, 0), (1, 2)}
+
+
+def graph():
+    ops, acc, cur = [], {}, [0.0]
+
+    def add(q, dur, fn, R, Wr, sem=None, inc=1, lat=0.0, deps=(), pr=0.0):
+        i = len(ops)
+        d = set(deps)
+        for lst, isw in ((R, False), (Wr, True)):
+            for (b, lo, hi) in lst:
+                for (k, kq, klo, khi, kw) in acc.get(b, []):
+                    if lo < khi and klo < hi and (isw or kw):
+                        d.add(k)
+                    elif b in BANKS and kq != q:
+                        d.add(k)
+        for lst, isw in ((R, False), (Wr, True)):
+            for (b, lo, hi) in lst:
+                old = acc.setdefault(b, [])
+                if isw and b not in BANKS:
+                    old[:] = [x for x in old if x[0] == i or not (lo <= x[2] and x[3] <= hi)]
+                old.append((i, q, lo, hi, isw))
+        ops.append({"q": q, "dur": dur, "fn": fn, "deps": d, "sem": sem, "inc": inc, "lat": lat, "pr": pr + cur[0]})
+        return i
+
+    def ap(T, x):
+        return T[x[0]][:, x[1]:x[2]]
+
+    def vdur(n, k=1.0):
+        return max(64.0, n * k) * VC + OV
+
+    def insb(x):
+        return x[0] not in BANKS
+
+    def tt(out, a, b, op, ind=None):
+        n = out[2] - out[1]
+        if ind is None:
+            f = lambda g, T, e: g.vector.tensor_tensor(ap(T, out), ap(T, a), ap(T, b), op)
+            return add("V", vdur(n, 2.0 if insb(a) and insb(b) else 1.0), f, [a, b], [out])
+        f = lambda g, T, e: g.vector.tensor_tensor(ap(T, out), ap(T, a).indirect(ap(T, ind)), ap(T, b), op)
+        return add("V", 50 + n * VG * VC, f, [a, b, ind], [out])
+
+    def ts(out, a, s1, op0, s2=None, op1=None):
+        R = [a] + [s for s in (s1, s2) if isinstance(s, tuple)]
+
+        def f(g, T, e):
+            v1 = ap(T, s1) if isinstance(s1, tuple) else s1
+            v2 = ap(T, s2) if isinstance(s2, tuple) else s2
+            if op1 is None:
+                return g.vector.tensor_scalar(ap(T, out), ap(T, a), v1, None, op0)
+            return g.vector.tensor_scalar(ap(T, out), ap(T, a), v1, v2, op0, op1)
+        return add("V", vdur(out[2] - out[1]), f, R, [out])
+
+    def cp(out, a):
+        return add("V", vdur(out[2] - out[1]), lambda g, T, e: g.vector.tensor_copy(ap(T, out), ap(T, a)), [a], [out])
+
+    def scat(win, ind, src):
+        return add("V", 50 + (src[2] - src[1]) * 3 * VC,
+                   lambda g, T, e: g.vector.tensor_copy(ap(T, win).indirect(ap(T, ind)), ap(T, src)), [src, ind], [win])
+
+    def ms(out, v):
+        return add("V", vdur(out[2] - out[1]), lambda g, T, e: g.vector.memset(ap(T, out), v), [], [out])
+
+    def sa(out, a, func, scale=1.0, bias=0.0, ind=None):
+        n = out[2] - out[1]
+        R = [a] + ([ind] if ind else []) + ([bias] if isinstance(bias, tuple) else [])
+
+        def f(g, T, e):
+            src = ap(T, a).indirect(ap(T, ind)) if ind else ap(T, a)
+            if func is F.Copy:
+                return g.scalar.activation(ap(T, out), src, func)
+            return g.scalar.activation(ap(T, out), src, func, bias=ap(T, bias) if isinstance(bias, tuple) else bias, scale=scale)
+        return add("S", (65 + n * VGS * VC) if ind else (max(64.0, n) * VC + 60), f, R, [out])
+
+    def sm(out, a, col):
+        return add("S", max(64.0, out[2] - out[1]) * VC + 60,
+                   lambda g, T, e: g.scalar.activation(ap(T, out), ap(T, a), F.Copy, scale=ap(T, col)), [a, col], [out])
+
+    def pas(out, w, src):
+        bank, lo, hi = out
+        name, a, b = src
+
+        def f(g, T, e):
+            r = None
+            for j in range(16):
+                r = g.tensor.matmul(T[bank][:, lo:hi], T[w][:, 15 - j:143 - j], T[name][:, a + j:b:16], j == 0, j == 15)
+            return r
+        return add("T", 16 * 64 * PC + 60, f, [(w, 0, 143), src], [out])
+
+    def mm(out, *pairs):
+        def f(g, T, e):
+            r = None
+            for k, (l, x) in enumerate(pairs):
+                r = g.tensor.matmul(ap(T, out), ap(T, l), ap(T, x), k == 0, k == len(pairs) - 1)
+            return r
+        return add("T", len(pairs) * max(out[2] - out[1], 64) * PC + 60, f, [p[0] for p in pairs] + [p[1] for p in pairs], [out])
+
+    def gi(out, pattern, base, cm, flag):
+        def f(g, T, e):
+            if flag:
+                return g.iota(ap(T, out), pattern, base, cm, allow_small_or_imprecise_dtypes=True)
+            return g.iota(ap(T, out), pattern, base, cm)
+        return add("G", 130 + (out[2] - out[1]) * 2 * VC, f, [], [out])
+
+    def gs(out, a, pattern, op, base, cm):
+        return add("G", 170 + 2 * VC * (out[2] - out[1]),
+                   lambda g, T, e: g.affine_select(ap(T, out), ap(T, a), pattern, op, 0.0, base, cm), [a], [out])
+
+    def full(n):
+        return (n, 0, SCRATCH[n][1][1])
+
+    def c_(n, c, lo=0, hi=None):
+        w = SCRATCH[n][1][1] // NC
+        return (n, c * w + lo, c * w + (w if hi is None else hi))
+
+    def ldq(c, s, q):
+        a = c * CH + 128 * s
+
+        def f(g, T, e):
+            return (g.sync if q == "Y" else g.scalar).dma_start(T.qa[:, a:a + 128], T.qs[:, 384 * s + 128 * c:384 * s + 128 * c + 128])
+        add(q, 60, f, [], [("qa", a, a + 128)], sem="lq%d" % c, inc=16, lat=2500, pr=1e6 - c * 1e4)
+
+    add("Y", 60, lambda g, T, e: g.sync.dma_start(T.wts[:, :], T.wt[:, :]), [], [full("wts")], sem="lw", inc=16, lat=2000, pr=5e6)
+    for c in range(NC):
+        for s in range(8):
+            ldq(c, s, "S" if c == 0 and s >= 4 else "Y")
+        if c == 0:
+            add("S", 60, lambda g, T, e: g.scalar.dma_start(T.mk0[:, :], T.mk[:, :]), [], [full("mk0")], sem="lm0", inc=16,
+                lat=7000, pr=5e5)
+    add("Y", 60, lambda g, T, e: g.sync.dma_start(T.mk1[:, 0:W], T.mk[:, :]), [], [("mk1", 0, W)], sem="lm1", inc=16, lat=7000)
+
+    gi(full("ip"), [[0, 1]], 0, 1, False)
+    ms(full("ones"), 1.0)
+    gs(full("z8a"), ("ones", 0, 8), [[-16, 8]], A.is_ge, 0, 1)
+    gs(full("z8"), full("z8a"), [[16, 8]], A.is_ge, 15, -1)
+    gs(full("idw"), full("ones"), [[1, 132]], A.is_equal, -2, -1)
+    gi(full("mrow"), [[0, 4], [1, 16]], 0, 0, True)
+    ts(full("i16"), full("ip"), 15, A.bitwise_and)
+    cp(full("icol"), full("i16"))
+    ms(full("bm"), 0.0)
+    add("V", 84, lambda g, T, e: g.vector.tensor_copy(T.bm[:, 15:128:16], T.z8[:, :]), [full("z8")], [full("bm")])
+    for n, op, v in (("m12", A.is_lt, 12.0), ("c12", A.is_equal, 12.0), ("c13", A.is_equal, 13.0), ("c14", A.is_equal, 14.0),
+                     ("ge13", A.is_ge, 13.0), ("ge14", A.is_ge, 14.0)):
+        ts(full(n), full("icol"), v, op)
+    cp(full("wtf"), full("wts"))
+    for k in range(3):
+        sm(full("WR%d" % k), full("bm"), full("c1%d" % (2 + k)))
+    sm(full("WX"), full("bm"), ("wtf", 0, 1))
+    sm(full("WY"), full("bm"), ("wtf", 1, 2))
+    cp(full("ident"), ("idw", 2, 130))
+    ts(full("nident"), ("idw", 2, 130), -1.0, A.mult)
+    ts(full("thv"), full("mrow"), full("icol"), A.is_gt, full("m12"), A.mult)
+    ts(full("ths"), full("thv"), 256.0, A.mult, -256.0, A.add)
+    sa(full("sil"), full("icol"), F.Silu, scale=-SL, bias=-SL)
+    ts(full("wc"), full("sil"), -1.5 * BIG, A.mult, full("m12"), A.mult)
+    sm(full("WE"), full("bm"), full("wc"))
+    ts(full("tha"), full("mrow"), 3.0, A.add, full("icol"), A.is_gt)
+    ts(full("thb"), full("mrow"), 0.0, A.is_gt, full("m12"), A.mult)
+    tt(full("th3"), full("tha"), full("thb"), A.mult)
+
+    def edit_constants():
+        gi(full("trow"), [[0, 2], [1, 128]], 0, 0, True)
+        gi(full("t16a"), [[0, 2], [16, 8]], 0, 0, True)
+        gi(full("iot"), [[256, 8208]], 0, 0, True)
+        ts(full("t16"), full("t16a"), full("icol"), A.add)
+        ts(full("dump16"), full("t16"), 8192.0, A.add)
+        sm(full("isym"), ("idw", 2, 130), full("m12"))
+        sm(full("sh1"), ("idw", 3, 131), full("ge13"))
+        sm(full("sh2"), ("idw", 4, 132), full("ge14"))
+        ts(full("sel1"), ("mrow", 0, 16), 2.0, A.is_equal)
+        ts(full("sel2"), ("mrow", 0, 16), 1.0, A.is_equal)
+        sm(full("mt"), ("mrow", 0, 16), full("c12"))
+        ts(full("mid"), full("icol"), 15.0, A.is_lt)
+        tt(full("wcm"), full("mid"), full("m12"), A.subtract)
+        sm(full("spa"), ("idw", 1, 129), full("wcm"))
+        tt(full("spl"), full("spa"), full("isym"), A.add)
+
+    def under(rd, c, st, q):
+        ml = c_("ml", c)
+        if (rd, c, st) in Z_V:
+            tt(c_("zz", c), full("thv"), c_(q, c), A.mult, ind=ml)
+            return
+        sa(c_("rr", c), full("ths"), F.Copy, ind=ml)
+        for h in (0, 512):
+            mm(("pw%d" % c, 0, 512), (full("ident"), c_(q, c, h, h + 512)), (full("ident"), c_("rr", c, h, h + 512)))
+            sa(c_("zz", c, h, h + 512), ("pw%d" % c, 0, 512), F.Relu)
+
+    def diff(c, out, mk, q, ind, byS):
+        if not byS:
+            tt(out, mk, c_(q, c), A.subtract, ind=ind)
+            return
+        sa(c_("rr", c), mk, F.Copy, ind=ind)
+        for h in (0, 512):
+            mm(("pw%d" % c, 0, 512), (full("ident"), c_("rr", c, h, h + 512)), (full("nident"), c_(q, c, h, h + 512)))
+            sa((out[0], out[1] + h, out[1] + h + 512), ("pw%d" % c, 0, 512), F.Copy)
+
+    def search(rd, c):
+        q = "qa" if rd == 0 else "qb"
+        mk = ("mk0" if rd == 0 else "mk1", 0, W)
+        pn, pw = "pn%d" % c, "pw%d" % c
+        u2, R0, R1, ky = (pn, 64, 128), (pn, 128, 192), (pn, 192, 256), (pn, 448, 512)
+        tA, tB = ("vp", c * 128, c * 128 + 64), ("vp", c * 128 + 64, c * 128 + 128)
+        hit = c_("hit", c)
+        rq = lambda k: c_("rq", c, NN * k, NN * k + NN)
+        pas((pn, 256, 320), "WR0", c_(q, c))
+        cp(c_("ml", c), (pn, 256, 320))
+        sa(rq(0), (pn, 256, 320), F.Copy)
+        for st in range(S):
+            m = rq(0) if st == 0 else c_("m%d" % (st + 1), c)
+            under(rd, c, st, q)
+            sa(c_("w97", c), m, F.Identity, scale=97.0)
+            sa(ky, m, F.Identity, scale=8192.0, bias=float((st + 1) << 17))
+            sa(c_("thr0", c), m, F.Silu, scale=-SL)
+            sa(c_("thr", c), c_("thr0", c), F.Abs, scale=BIG)
+            pas((pn, 0, 64), "WX", c_("zz", c))
+            pas(u2, "WY", c_("zz", c))
+            cp(c_("ui", c), (pn, 0, 128))
+            ts(c_("ac", c), c_("ui", c), 4095, A.bitwise_and)
+            tt(tA, u2, c_("w97", c), A.add)
+            tt(c_("pp", c), c_("ac", c, 0, NN), c_("ac", c, NN, 2 * NN), A.mult)
+            ts(c_("kk", c), c_("pp", c), 5, A.arith_shift_right)
+            tt(c_("ss", c), tA, c_("kk", c), A.add)
+            ts(c_("hi", c), c_("ss", c), W - 1, A.bitwise_and)
+            cp(c_("hl", c), c_("hi", c))
+            tt(ky, ky, c_("hi", c), A.add)
+            if rd == 0 and c == 0:
+                x8 = ("act", 8 * st, 8 * st + 8)
+                ts(x8, (m[0], m[1], m[1] + 8), 0.0, A.is_gt)
+                tt(("ka", 8 * st, 8 * st + 8), (pn, 448, 456), x8, A.mult)
+            diff(c, c_("dd", c), mk, q, c_("hl", c), (rd, c, st) in D_S)
+            if st == 0:
+                for k in (1, 2):
+                    pas((pn, 256 + 64 * k, 320 + 64 * k), "WR%d" % k, c_(q, c))
+                sa(c_("rq", c, NN, 3 * NN), (pn, 320, 448), F.Copy)
+                tt(c_("xx", c), (pn, 256, 384), c_("rq", c, NN, 3 * NN), A.subtract)
+            pas((pw, 0, 64), "WE", c_("dd", c))
+            if st < 2:
+                pas(R0, "WR0", c_("dd", c))
+            if st < 1:
+                pas(R1, "WR1", c_("dd", c))
+            sa((pw, 64, 128), (pw, 0, 64), F.Abs)
+            tt(hit, (pw, 64, 128), c_("thr", c), A.is_lt)
+            if st < 2:
+                nx = c_("m%d" % (st + 2), c)
+                if st == 0:
+                    x, old = c_("xx", c, 0, NN), rq(1)
+                else:
+                    x, old = c_("x2", c), c_("n2", c)
+                    tt(x, rq(0), old, A.subtract)
+                tt(tB, R0, x, A.add)
+                tt(tB, tB, hit, A.mult)
+                tt(nx, tB, old, A.add)
+                cp(c_("ml", c), nx)
+            if st == 0:
+                tt(c_("kb", c), ky, hit, A.mult)
+                tt(tA, R1, c_("xx", c, NN, 2 * NN), A.add)
+                tt(tA, tA, hit, A.mult)
+                tt(c_("n2", c), tA, rq(2), A.add)
+            else:
+                tt(tA, ky, hit, A.mult)
+                tt(c_("kb", c), tA, c_("kb", c), A.max)
+
+    def learn(rd, c):
+        q = "qa" if rd == 0 else "qb"
+        nw = "nwa" if rd == 0 else "nwb"
+        mk = ("mk0" if rd == 0 else "mk1", 0, W)
+        cp(c_("ki", c), c_("kb", c))
+        ts(c_("bi", c), c_("ki", c), W - 1, A.bitwise_and)
+        cp(c_("bl", c), c_("bi", c))
+        diff(c, c_("ld", c), mk, q, c_("bl", c), (rd, c) in L_S)
+        ts(c_("mbi", c), c_("ki", c), 13, A.arith_shift_right)
+        cp(c_("mbl", c), c_("mbi", c))
+        tt(c_("lm", c), full("th3"), c_("ld", c), A.mult, ind=c_("mbl", c))
+        for h in (0, 512):
+            mm(("pw%d" % c, 0, 512), (full("ident"), c_(q, c, h, h + 512)), (full("ident"), c_("lm", c, h, h + 512)))
+            sa(c_(nw, c, h, h + 512), ("pw%d" % c, 0, 512), F.Copy)
+
+    def move(c):
+        def f(g, T, e):
+            core, rank, topo = e
+            moves, k = [], 0
+            for d in range(1, 8):
+                s = (rank + d) % 8
+                dst = T.cores[s]
+                en = topo.engines(core, dst)
+                if topo.chip(dst) == topo.chip(core):
+                    eng = en[-1]
+                else:
+                    eng = (en[0::2] + en[1::2])[k]
+                    k += 1
+                ad = topo.addr(dst)
+                moves.append(RemoteDMATransfer(
+                    dst_ids=[DstId(rid=ad[0], pnc=ad[1])], dma_engine_mask=1 << eng, remote_sem=T.sem["arr%d" % c],
+                    src=T.nwa[:, c * CH + 128 * s:c * CH + 128 * s + 128],
+                    dst=T.qb[:, c * CH + 128 * rank:c * CH + 128 * rank + 128]))
+            return g.remote_dma_fused(moves, local_sem=T.sem["snt%d" % c])
+        i = add("G", 1500, f, [c_("nwa", c)], [], sem="none%d" % c, inc=0)
+        add("arr%d" % c, 0, None, [], [c_("qb", c)], sem="arr%d" % c, inc=7, lat=7000, deps=(i,))
+
+        def f2(g, T, e):
+            a = c * CH + 128 * e[1]
+            return g.sync.dma_start(T.qb[:, a:a + 128], T.nwa[:, a:a + 128])
+        k = add("Y", 60, f2, [c_("nwa", c)], [], sem="slf%d" % c, inc=16, lat=2500)
+        acc["qb"].append((k, "Y", c * CH, c * CH + CH, True))
+
+    def edits():
+        e8 = lambda n: c_(n, 0, 0, 8)
+        a8 = lambda n, k: (n, 8 * k, 8 * k + 8)
+        tt(full("kam"), a8("ka", 0), a8("ka", 1), A.max)
+        tt(full("kam"), full("kam"), a8("ka", 2), A.max)
+        cp(full("kai"), full("kam"))
+        ts(full("fi"), full("kai"), W - 1, A.bitwise_and)
+        ts(full("mfi"), full("kai"), 13, A.arith_shift_right, 15, A.bitwise_and)
+        ts(full("sbi"), e8("ki"), 17, A.arith_shift_right)
+        cp(full("sbl"), full("sbi"))
+        cp(full("mfl"), full("mfi"))
+        tt(full("ed1"), full("kam"), e8("kb"), A.is_gt)
+        ts(full("ed0"), e8("kb"), 0.0, A.is_gt)
+        for k in (0, 1):
+            tt(a8("ed", k), full("ed1"), full("ed0"), A.mult)
+        ts(a8("fbm", 0), full("fi"), -8192.0, A.add)
+        ts(a8("fbm", 1), e8("bi"), -8192.0, A.add)
+        tt(full("fbe"), full("fbm"), full("ed"), A.mult)
+        ts(full("flu"), full("fbe"), 8192.0, A.add)
+        ts(full("nb"), full("fbe"), -256.0, A.mult, -2097152.0, A.add)
+        tt(full("krow"), full("iot"), full("trow"), A.add, ind=full("flu"))
+        for k in range(16):
+            h = 128 * (k // 8)
+            sa(("dk", 128 * k, 128 * k + 128), ("krow", h, h + 128), F.Identity, bias=("nb", k, k + 1))
+            add("V", vdur(128), lambda g, T, e, k=k: g.vector.tensor_reduce(
+                T.first[:, k:k + 1], T.dk[:, 128 * k:128 * k + 128], AxisListType.X, A.min, apply_absolute_value=True),
+                [("dk", 128 * k, 128 * k + 128)], [("first", k, k + 1)])
+        tt(full("win"), full("first"), full("t16"), A.is_equal)
+        tt(full("win"), full("win"), full("ed"), A.mult)
+        tt(full("gg"), full("fbm"), full("t16"), A.subtract)
+        tt(full("gg"), full("gg"), full("win"), A.mult)
+        tt(full("tgt"), full("gg"), full("dump16"), A.add)
+        cp(full("tgu"), full("tgt"))
+        sa(full("g0"), ("mk0", 0, W), F.Copy, ind=e8("bl"))
+        tt(full("ga1"), full("sel1"), full("g0"), A.mult, ind=full("sbl"))
+        tt(full("ga2"), full("sel2"), full("g0"), A.mult, ind=full("sbl"))
+        mm(("pe", 0, 128), (full("sh1"), full("ga1")), (full("sh2"), full("ga2")), (full("isym"), ("qa", 0, 128)))
+        sa(full("wnew"), ("pe", 0, 128), F.Copy)
+        scat(full("mk1"), ("tgu", 0, 8), full("wnew"))
+        sa(full("g1"), ("mk1", 0, W), F.Copy, ind=e8("bl"))
+        sa(full("mfw"), full("mt"), F.Copy, ind=full("mfl"))
+        mm(("pe", 0, 128), (full("spl"), full("g1")), (full("ident"), full("mfw")))
+        sa(full("snew"), ("pe", 0, 128), F.Copy)
+        scat(full("mk1"), ("tgu", 8, 16), full("snew"))
+
+    def blocks(c):
+        ts(c_("ybx", c), c_("kb", c), 0.0, A.is_equal, -1.0, A.mult)
+        add("V", vdur(64, 2), lambda g, T, e: g.vector.tensor_tensor(T.yby[:, :, 8 * c:8 * c + 8], ap(T, c_("ybx", c)),
+            ap(T, c_("bi", c)), A.add), [c_("ybx", c), c_("bi", c)], [("yby", 64 * c, 64 * c + 64)])
+        if c == NC - 1:
+            add("Y", 60, lambda g, T, e: g.sync.dma_start(T.yb[:, :], T.yby[:, :, :]),
+                [("yby", 0, 192)], [], sem="lyb", inc=16, lat=2500)
+
+    def store(c):
+        for s in range(8):
+            q = "S" if c == NC - 1 and s >= 6 else "Y"
+            a = c * CH + 128 * s
+
+            def f(g, T, e, a=a, s=s, q=q):
+                return (g.sync if q == "Y" else g.scalar).dma_start(
+                    T.yq[:, 384 * s + 128 * c:384 * s + 128 * c + 128], T.nwb[:, a:a + 128])
+            add(q, 60, f, [("nwb", a, a + 128)], [], sem="out%d" % c, inc=16, lat=2500)
+
+    for c in range(NC):
+        cur[0] = BIAS[c]
+        search(0, c)
+        learn(0, c)
+        move(c)
+    cur[0] = BIAS[3]
+    edit_constants()
+    cur[0] = BIAS[4]
+    edits()
+    for c in range(NC):
+        cur[0] = BIAS[5 + c]
+        search(1, c)
+        learn(1, c)
+        blocks(c)
+        store(c)
+    return ops
+
+
+QSEM = {"T": "sT", "V": "sV", "S": "sS", "G": "sG"}
+
+
+def schedule(ops):
+    n = len(ops)
+    kids = [[] for _ in range(n)]
+    need = [len(o["deps"]) for o in ops]
+    for i, o in enumerate(ops):
+        for d in o["deps"]:
+            kids[d].append(i)
+    tail = [0.0] * n
+    for i in range(n - 1, -1, -1):
+        tail[i] = ops[i]["dur"] + ops[i]["lat"] + max([tail[k] + WAKE for k in kids[i]] or [0.0])
+    free, ready, est, done = {}, {}, [0.0] * n, [0.0] * n
+    for i in range(n):
+        ready.setdefault(ops[i]["q"], [])
+        free[ops[i]["q"]] = 0.0
+        if need[i] == 0:
+            ready[ops[i]["q"]].append(i)
+    order = []
+    for _ in range(n):
+        best = None
+        for q, lst in ready.items():
+            if lst:
+                t = max(free[q], min(est[i] for i in lst))
+                if best is None or t < best[0]:
+                    best = (t, q)
+        t, q = best
+        i = max((i for i in ready[q] if est[i] <= t), key=lambda i: (tail[i] + ops[i]["pr"], -i))
+        ready[q].remove(i)
+        free[q] = t + ops[i]["dur"]
+        done[i] = free[q] + ops[i]["lat"]
+        order.append(i)
+        for k in kids[i]:
+            est[k] = max(est[k], done[i] + WAKE)
+            need[k] -= 1
+            if need[k] == 0:
+                ready[ops[k]["q"]].append(k)
+    return order, max(done), done
+
+
+PLAN = {}
+
+
+def rank_program(g, core, T, topo):
+    rank = T.rank_of(core)
+    if rank is None:
+        return
+    if not PLAN:
+        PLAN["ops"] = graph()
+        PLAN["order"] = schedule(PLAN["ops"])[0]
+    ops, order = PLAN["ops"], PLAN["order"]
+    env = (core, rank, topo)
+    eng = {"T": g.tensor, "V": g.vector, "S": g.scalar, "G": g, "Y": g.sync}
+    total = {}
+    for o in ops:
+        if o["sem"] and o["inc"]:
+            total[o["sem"]] = total.get(o["sem"], 0) + o["inc"]
+    count, stamp, clock, known = {}, {}, {}, {}
+    for i in order:
+        o = ops[i]
+        q = o["q"]
+        kn = known.setdefault(q, {})
+        want = {}
+        for d in o["deps"]:
+            s, v = stamp[d]
+            if kn.get(s, 0) < v:
+                want[s] = max(want.get(s, 0), v)
+        for s in sorted(want, key=lambda s: -len(clock[(s, want[s])])):
+            v = want[s]
+            if kn.get(s, 0) >= v:
+                continue
+            if o["fn"] is not None and not s.startswith("none"):
+                eng[q].wait_ge(T.sem[s], v)
+            kn[s] = max(kn.get(s, 0), v)
+            for s2, v2 in clock[(s, v)].items():
+                kn[s2] = max(kn.get(s2, 0), v2)
+        ins = o["fn"](g, T, env) if o["fn"] is not None else None
+        if o["sem"] is None:
+            s = QSEM[q]
+            count[s] = count.get(s, 0) + 1
+            ins.then_inc(T.sem[s], 1)
+            v = count[s]
+            prev = clock.get((s, v - 1), {})
+        else:
+            s = o["sem"]
+            v = total.get(s, 1)
+            if ins is not None and o["inc"]:
+                ins.then_inc(T.sem[s], o["inc"])
+            prev = clock.get((s, v), {})
+        stamp[i] = (s, v)
+        ck = {}
+        if not s.startswith("arr"):
+            ck = dict(prev)
+            for s2, v2 in kn.items():
+                ck[s2] = max(ck.get(s2, 0), v2)
+        clock[(s, v)] = ck
+    for s in SEMAPHORES:
+        if s in count:
+            g.wait_ge(T.sem[s], count[s])
+        else:
+            g.wait_ge(T.sem[s], total[s] if s in total else 7)

@@ -36,15 +36,20 @@ SEMAPHORES = ["sT", "sV", "sS", "sG", "lw", "lm0", "lm1", "lyb"]
 for _c in range(NC):
     SEMAPHORES += ["lq%d" % _c, "slf%d" % _c, "arr%d" % _c, "snt%d" % _c, "out%d" % _c]
 
-VC, PC, VG, VGS, OV, WAKE = 1.0, 0.5, 1.5, 1.5, 20.0, 60.0
-BIAS = [91000.0, 6000.0, 92000.0, -297000.0, 0.0, 10000.0, 3000.0, 3000.0]
-Z_V = {(0, 0, 1), (0, 0, 2), (0, 1, 0), (0, 2, 0), (0, 2, 1), (1, 0, 0), (1, 0, 2), (1, 1, 0), (1, 1, 1), (1, 1, 2), (1, 2, 0)}
-D_S = {(1, 0, 1)}
-L_S = {(1, 0), (1, 2)}
+VC, PC, VG, VGS, OV, WAKE = 0.9545, 0.575, 1.5, 1.5, 20.0, 110.0
+BIAS = {"k": -1058e3, "e": 354e3}
+for _k, _v in (("00", (184, -129, -1279, 631)), ("01", (-1, 1099, 683, 606)), ("02", (615, 632, -124, 711)),
+               ("10", (1096, -254, 1530, -251)), ("11", (-293, 381, -1481, -1093)), ("12", (-816, -872, -293, 4))):
+    for _i in range(4):
+        BIAS[_k + str(_i)] = _v[_i] * 1e3
+Z_V = {(0, 0, 0), (0, 0, 1), (0, 0, 2), (0, 1, 0), (0, 1, 2), (0, 2, 0), (0, 2, 1), (0, 2, 2), (1, 0, 0), (1, 0, 1), (1, 0, 2),
+       (1, 1, 0), (1, 1, 1), (1, 1, 2), (1, 2, 0), (1, 2, 1)}
+D_S = {(0, 0, 1), (0, 0, 2), (1, 0, 2), (1, 1, 2)}
+L_S = {(0, 0), (1, 0)}
 
 
 def graph():
-    ops, acc, cur = [], {}, [0.0]
+    ops, acc, cur = [], {}, [""]
 
     def add(q, dur, fn, R, Wr, sem=None, inc=1, lat=0.0, deps=(), pr=0.0):
         i = len(ops)
@@ -62,7 +67,7 @@ def graph():
                 if isw and b not in BANKS:
                     old[:] = [x for x in old if x[0] == i or not (lo <= x[2] and x[3] <= hi)]
                 old.append((i, q, lo, hi, isw))
-        ops.append({"q": q, "dur": dur, "fn": fn, "deps": d, "sem": sem, "inc": inc, "lat": lat, "pr": pr + cur[0]})
+        ops.append({"q": q, "dur": dur, "fn": fn, "deps": d, "sem": sem, "inc": inc, "lat": lat, "pr": pr, "tag": cur[0]})
         return i
 
     def ap(T, x):
@@ -160,15 +165,15 @@ def graph():
 
         def f(g, T, e):
             return (g.sync if q == "Y" else g.scalar).dma_start(T.qa[:, a:a + 128], T.qs[:, 384 * s + 128 * c:384 * s + 128 * c + 128])
-        add(q, 60, f, [], [("qa", a, a + 128)], sem="lq%d" % c, inc=16, lat=2500, pr=1e6 - c * 1e4)
+        add(q, 60, f, [], [("qa", a, a + 128)], sem="lq%d" % c, inc=16, lat=2500, pr=1e7 - c * 1e4)
 
-    add("Y", 60, lambda g, T, e: g.sync.dma_start(T.wts[:, :], T.wt[:, :]), [], [full("wts")], sem="lw", inc=16, lat=2000, pr=5e6)
+    add("Y", 60, lambda g, T, e: g.sync.dma_start(T.wts[:, :], T.wt[:, :]), [], [full("wts")], sem="lw", inc=16, lat=2000, pr=5e7)
     for c in range(NC):
         for s in range(8):
             ldq(c, s, "S" if c == 0 and s >= 4 else "Y")
         if c == 0:
             add("S", 60, lambda g, T, e: g.scalar.dma_start(T.mk0[:, :], T.mk[:, :]), [], [full("mk0")], sem="lm0", inc=16,
-                lat=7000, pr=5e5)
+                lat=7000, pr=5e6)
     add("Y", 60, lambda g, T, e: g.sync.dma_start(T.mk1[:, 0:W], T.mk[:, :]), [], [("mk1", 0, W)], sem="lm1", inc=16, lat=7000)
 
     gi(full("ip"), [[0, 1]], 0, 1, False)
@@ -222,8 +227,8 @@ def graph():
         if (rd, c, st) in Z_V:
             tt(c_("zz", c), full("thv"), c_(q, c), A.mult, ind=ml)
             return
-        sa(c_("rr", c), full("ths"), F.Copy, ind=ml)
         for h in (0, 512):
+            sa(c_("rr", c, h, h + 512), full("ths"), F.Copy, ind=c_("ml", c, h // 16, h // 16 + 32))
             mm(("pw%d" % c, 0, 512), (full("ident"), c_(q, c, h, h + 512)), (full("ident"), c_("rr", c, h, h + 512)))
             sa(c_("zz", c, h, h + 512), ("pw%d" % c, 0, 512), F.Relu)
 
@@ -231,8 +236,8 @@ def graph():
         if not byS:
             tt(out, mk, c_(q, c), A.subtract, ind=ind)
             return
-        sa(c_("rr", c), mk, F.Copy, ind=ind)
         for h in (0, 512):
+            sa(c_("rr", c, h, h + 512), mk, F.Copy, ind=(ind[0], ind[1] + h // 16, ind[1] + h // 16 + 32))
             mm(("pw%d" % c, 0, 512), (full("ident"), c_("rr", c, h, h + 512)), (full("nident"), c_(q, c, h, h + 512)))
             sa((out[0], out[1] + h, out[1] + h + 512), ("pw%d" % c, 0, 512), F.Copy)
 
@@ -244,10 +249,12 @@ def graph():
         tA, tB = ("vp", c * 128, c * 128 + 64), ("vp", c * 128 + 64, c * 128 + 128)
         hit = c_("hit", c)
         rq = lambda k: c_("rq", c, NN * k, NN * k + NN)
+        cur[0] = "%d%d0" % (rd, c)
         pas((pn, 256, 320), "WR0", c_(q, c))
         cp(c_("ml", c), (pn, 256, 320))
         sa(rq(0), (pn, 256, 320), F.Copy)
         for st in range(S):
+            cur[0] = "%d%d%d" % (rd, c, st)
             m = rq(0) if st == 0 else c_("m%d" % (st + 1), c)
             under(rd, c, st, q)
             sa(c_("w97", c), m, F.Identity, scale=97.0)
@@ -306,14 +313,15 @@ def graph():
         q = "qa" if rd == 0 else "qb"
         nw = "nwa" if rd == 0 else "nwb"
         mk = ("mk0" if rd == 0 else "mk1", 0, W)
+        cur[0] = "%d%d3" % (rd, c)
         cp(c_("ki", c), c_("kb", c))
         ts(c_("bi", c), c_("ki", c), W - 1, A.bitwise_and)
         cp(c_("bl", c), c_("bi", c))
         diff(c, c_("ld", c), mk, q, c_("bl", c), (rd, c) in L_S)
         ts(c_("mbi", c), c_("ki", c), 13, A.arith_shift_right)
         cp(c_("mbl", c), c_("mbi", c))
-        tt(c_("lm", c), full("th3"), c_("ld", c), A.mult, ind=c_("mbl", c))
         for h in (0, 512):
+            tt(c_("lm", c, h, h + 512), full("th3"), c_("ld", c, h, h + 512), A.mult, ind=c_("mbl", c, h // 16, h // 16 + 32))
             mm(("pw%d" % c, 0, 512), (full("ident"), c_(q, c, h, h + 512)), (full("ident"), c_("lm", c, h, h + 512)))
             sa(c_(nw, c, h, h + 512), ("pw%d" % c, 0, 512), F.Copy)
 
@@ -367,11 +375,11 @@ def graph():
         ts(full("nb"), full("fbe"), -256.0, A.mult, -2097152.0, A.add)
         tt(full("krow"), full("iot"), full("trow"), A.add, ind=full("flu"))
         for k in range(16):
-            h = 128 * (k // 8)
-            sa(("dk", 128 * k, 128 * k + 128), ("krow", h, h + 128), F.Identity, bias=("nb", k, k + 1))
-            add("V", vdur(128), lambda g, T, e, k=k: g.vector.tensor_reduce(
-                T.first[:, k:k + 1], T.dk[:, 128 * k:128 * k + 128], AxisListType.X, A.min, apply_absolute_value=True),
-                [("dk", 128 * k, 128 * k + 128)], [("first", k, k + 1)])
+            h, n = 128 * (k // 8), 16 * (k % 8 + 1)
+            sa(("dk", 128 * k, 128 * k + n), ("krow", h, h + n), F.Identity, bias=("nb", k, k + 1))
+            add("V", vdur(n), lambda g, T, e, k=k, n=n: g.vector.tensor_reduce(
+                T.first[:, k:k + 1], T.dk[:, 128 * k:128 * k + n], AxisListType.X, A.min, apply_absolute_value=True),
+                [("dk", 128 * k, 128 * k + n)], [("first", k, k + 1)])
         tt(full("win"), full("first"), full("t16"), A.is_equal)
         tt(full("win"), full("win"), full("ed"), A.mult)
         tt(full("gg"), full("fbm"), full("t16"), A.subtract)
@@ -409,16 +417,14 @@ def graph():
             add(q, 60, f, [("nwb", a, a + 128)], [], sem="out%d" % c, inc=16, lat=2500)
 
     for c in range(NC):
-        cur[0] = BIAS[c]
         search(0, c)
         learn(0, c)
         move(c)
-    cur[0] = BIAS[3]
+    cur[0] = "k"
     edit_constants()
-    cur[0] = BIAS[4]
+    cur[0] = "e"
     edits()
     for c in range(NC):
-        cur[0] = BIAS[5 + c]
         search(1, c)
         learn(1, c)
         blocks(c)
@@ -454,7 +460,7 @@ def schedule(ops):
                 if best is None or t < best[0]:
                     best = (t, q)
         t, q = best
-        i = max((i for i in ready[q] if est[i] <= t), key=lambda i: (tail[i] + ops[i]["pr"], -i))
+        i = max((i for i in ready[q] if est[i] <= t), key=lambda i: (tail[i] + ops[i]["pr"] + BIAS.get(ops[i]["tag"], 0.0), -i))
         ready[q].remove(i)
         free[q] = t + ops[i]["dur"]
         done[i] = free[q] + ops[i]["lat"]

from concourse.bass import DstId, RemoteDMATransfer
from concourse.mybir import AluOpType, AxisListType, ActivationFunctionType

A = AluOpType
F = ActivationFunctionType
W, NC, CH, NN, S = 8192, 3, 1024, 64, 3
BIG, SL = 2.0 ** 60, 7.6

SCRATCH, BANKS = {}, []


def _b(dtype, where, spec, k=1):
    for x in spec.split():
        n, w = x.split(":")
        SCRATCH[n] = (where, [128, k * int(w)], dtype)
        if where == "psum":
            BANKS.append(n)


_b("bfloat16", "sbuf", "mk0:8192 mk1:8320 wts:2 ones:132 idw:132 ident:128 nident:128 isym:128 sh1:128 sh2:128 spl:128 spa:128 "
   "z8a:8 z8:8 bm:143 WX:143 WY:143 WE:143 WR0:143 WR1:143 WR2:143 thv:64 ths:64 tha:64 thb:64 th3:64 sel1:16 sel2:16 "
   "mt:16 g0:128 ga1:128 ga2:128 wnew:128 g1:128 mfw:128 snew:128")
_b("int32", "sbuf", "ip:1 i16:1 kai:8 fi:8 mfi:8 sbi:8")
_b("uint16", "sbuf", "flu:16 tgu:16 sbl:8 mfl:8")
_b("float32", "sbuf", "icol:1 m12:1 sil:1 wc:1 c12:1 c13:1 c14:1 ge13:1 ge14:1 mid:1 wcm:1 wtf:2 mrow:64 iot:8208 trow:256 "
   "t16a:16 t16:16 dump16:16 act:24 ka:24 kam:8 ed1:8 ed0:8 ed:16 fbm:16 fbe:16 nb:16 krow:256 dk:2048 first:16 win:16 "
   "gg:16 tgt:16")
SCRATCH["yby"] = ("sbuf", [128, 8, 24], "float32")
_b("bfloat16", "sbuf", "qa:1024 qb:1024 rr:1024 zz:1024 dd:1024 ld:1024 lm:1024 nwa:1024 nwb:1024", NC)
_b("float32", "sbuf", "rq:192 xx:128 x2:64 n2:64 m2:64 m3:64 thr0:64 thr:64 w97:64 hit:64 kb:64 ybx:64", NC)
_b("int32", "sbuf", "ui:128 ac:128 pp:64 kk:64 ss:64 hi:64 ki:64 bi:64 mbi:64", NC)
_b("uint16", "sbuf", "ml:64 hl:64 bl:64 mbl:64", NC)
_b("float32", "psum", "pn0:512 pn1:512 pn2:512 pw0:512 pw1:512 pw2:512 vp:512 pe:512")

SEMAPHORES = ["sT", "sV", "sS", "sG", "lw", "lm0", "lm1", "lyb"]
for _c in range(NC):
    SEMAPHORES += ["lq%d" % _c, "slf%d" % _c, "arr%d" % _c, "snt%d" % _c, "out%d" % _c]

VC, PC, VG, VGS, OV, WAKE = 0.9545, 0.575, 1.5, 1.5, 20.0, 110.0
BIAS = {"k": -1058e3, "e": 354e3}
for _k, _v in (("00", (184, -129, -1279, 631)), ("01", (-1, 1099, 683, 606)), ("02", (615, 632, -124, 711)),
               ("10", (1096, -254, 1530, -251)), ("11", (-293, 381, -1481, -1093)), ("12", (-816, -872, -293, 4))):
    for _i in range(4):
        BIAS[_k + str(_i)] = _v[_i] * 1e3
Z_V = {(0, 0, 0), (0, 0, 1), (0, 0, 2), (0, 1, 0), (0, 1, 2), (0, 2, 0), (0, 2, 1), (0, 2, 2), (1, 0, 0), (1, 0, 1), (1, 0, 2),
       (1, 1, 0), (1, 1, 1), (1, 1, 2), (1, 2, 0), (1, 2, 1)}
D_S = {(0, 0, 1), (0, 0, 2), (1, 0, 2), (1, 1, 2)}
L_S = {(0, 0), (1, 0)}


def graph():
    ops, acc, cur = [], {}, [""]

    def add(q, dur, fn, R, Wr, sem=None, inc=1, lat=0.0, deps=(), pr=0.0):
        i = len(ops)
        d = set(deps)
        for lst, isw in ((R, False), (Wr, True)):
            for (b, lo, hi) in lst:
                for (k, kq, klo, khi, kw) in acc.get(b, []):
                    if lo < khi and klo < hi and (isw or kw):
                        d.add(k)
                    elif b in BANKS and kq != q:
                        d.add(k)
        for lst, isw in ((R, False), (Wr, True)):
            for (b, lo, hi) in lst:
                old = acc.setdefault(b, [])
                if isw and b not in BANKS:
                    old[:] = [x for x in old if x[0] == i or not (lo <= x[2] and x[3] <= hi)]
                old.append((i, q, lo, hi, isw))
        ops.append({"q": q, "dur": dur, "fn": fn, "deps": d, "sem": sem, "inc": inc, "lat": lat, "pr": pr, "tag": cur[0]})
        return i

    def ap(T, x):
        return T[x[0]][:, x[1]:x[2]]

    def vdur(n, k=1.0):
        return max(64.0, n * k) * VC + OV

    def insb(x):
        return x[0] not in BANKS

    def tt(out, a, b, op, ind=None):
        n = out[2] - out[1]
        if ind is None:
            f = lambda g, T, e: g.vector.tensor_tensor(ap(T, out), ap(T, a), ap(T, b), op)
            return add("V", vdur(n, 2.0 if insb(a) and insb(b) else 1.0), f, [a, b], [out])
        f = lambda g, T, e: g.vector.tensor_tensor(ap(T, out), ap(T, a).indirect(ap(T, ind)), ap(T, b), op)
        return add("V", 50 + n * VG * VC, f, [a, b, ind], [out])

    def ts(out, a, s1, op0, s2=None, op1=None):
        R = [a] + [s for s in (s1, s2) if isinstance(s, tuple)]

        def f(g, T, e):
            v1 = ap(T, s1) if isinstance(s1, tuple) else s1
            v2 = ap(T, s2) if isinstance(s2, tuple) else s2
            if op1 is None:
                return g.vector.tensor_scalar(ap(T, out), ap(T, a), v1, None, op0)
            return g.vector.tensor_scalar(ap(T, out), ap(T, a), v1, v2, op0, op1)
        return add("V", vdur(out[2] - out[1]), f, R, [out])

    def cp(out, a):
        return add("V", vdur(out[2] - out[1]), lambda g, T, e: g.vector.tensor_copy(ap(T, out), ap(T, a)), [a], [out])

    def scat(win, ind, src):
        return add("V", 50 + (src[2] - src[1]) * 3 * VC,
                   lambda g, T, e: g.vector.tensor_copy(ap(T, win).indirect(ap(T, ind)), ap(T, src)), [src, ind], [win])

    def ms(out, v):
        return add("V", vdur(out[2] - out[1]), lambda g, T, e: g.vector.memset(ap(T, out), v), [], [out])

    def sa(out, a, func, scale=1.0, bias=0.0, ind=None):
        n = out[2] - out[1]
        R = [a] + ([ind] if ind else []) + ([bias] if isinstance(bias, tuple) else [])

        def f(g, T, e):
            src = ap(T, a).indirect(ap(T, ind)) if ind else ap(T, a)
            if func is F.Copy:
                return g.scalar.activation(ap(T, out), src, func)
            return g.scalar.activation(ap(T, out), src, func, bias=ap(T, bias) if isinstance(bias, tuple) else bias, scale=scale)
        return add("S", (65 + n * VGS * VC) if ind else (max(64.0, n) * VC + 60), f, R, [out])

    def sm(out, a, col):
        return add("S", max(64.0, out[2] - out[1]) * VC + 60,
                   lambda g, T, e: g.scalar.activation(ap(T, out), ap(T, a), F.Copy, scale=ap(T, col)), [a, col], [out])

    def pas(out, w, src):
        bank, lo, hi = out
        name, a, b = src

        def f(g, T, e):
            r = None
            for j in range(16):
                r = g.tensor.matmul(T[bank][:, lo:hi], T[w][:, 15 - j:143 - j], T[name][:, a + j:b:16], j == 0, j == 15)
            return r
        return add("T", 16 * 64 * PC + 60, f, [(w, 0, 143), src], [out])

    def mm(out, *pairs):
        def f(g, T, e):
            r = None
            for k, (l, x) in enumerate(pairs):
                r = g.tensor.matmul(ap(T, out), ap(T, l), ap(T, x), k == 0, k == len(pairs) - 1)
            return r
        return add("T", len(pairs) * max(out[2] - out[1], 64) * PC + 60, f, [p[0] for p in pairs] + [p[1] for p in pairs], [out])

    def gi(out, pattern, base, cm, flag):
        def f(g, T, e):
            if flag:
                return g.iota(ap(T, out), pattern, base, cm, allow_small_or_imprecise_dtypes=True)
            return g.iota(ap(T, out), pattern, base, cm)
        return add("G", 130 + (out[2] - out[1]) * 2 * VC, f, [], [out])

    def gs(out, a, pattern, op, base, cm):
        return add("G", 170 + 2 * VC * (out[2] - out[1]),
                   lambda g, T, e: g.affine_select(ap(T, out), ap(T, a), pattern, op, 0.0, base, cm), [a], [out])

    def full(n):
        return (n, 0, SCRATCH[n][1][1])

    def c_(n, c, lo=0, hi=None):
        w = SCRATCH[n][1][1] // NC
        return (n, c * w + lo, c * w + (w if hi is None else hi))

    def ldq(c, s, q):
        a = c * CH + 128 * s

        def f(g, T, e):
            return (g.sync if q == "Y" else g.scalar).dma_start(T.qa[:, a:a + 128], T.qs[:, 384 * s + 128 * c:384 * s + 128 * c + 128])
        add(q, 60, f, [], [("qa", a, a + 128)], sem="lq%d" % c, inc=16, lat=2500, pr=1e7 - c * 1e4)

    add("Y", 60, lambda g, T, e: g.sync.dma_start(T.wts[:, :], T.wt[:, :]), [], [full("wts")], sem="lw", inc=16, lat=2000, pr=5e7)
    for c in range(NC):
        for s in range(8):
            ldq(c, s, "S" if c == 0 and s >= 4 else "Y")
        if c == 0:
            add("S", 60, lambda g, T, e: g.scalar.dma_start(T.mk0[:, :], T.mk[:, :]), [], [full("mk0")], sem="lm0", inc=16,
                lat=7000, pr=5e6)
    add("Y", 60, lambda g, T, e: g.sync.dma_start(T.mk1[:, 0:W], T.mk[:, :]), [], [("mk1", 0, W)], sem="lm1", inc=16, lat=7000)

    gi(full("ip"), [[0, 1]], 0, 1, False)
    ms(full("ones"), 1.0)
    gs(full("z8a"), ("ones", 0, 8), [[-16, 8]], A.is_ge, 0, 1)
    gs(full("z8"), full("z8a"), [[16, 8]], A.is_ge, 15, -1)
    gs(full("idw"), full("ones"), [[1, 132]], A.is_equal, -2, -1)
    gi(full("mrow"), [[0, 4], [1, 16]], 0, 0, True)
    ts(full("i16"), full("ip"), 15, A.bitwise_and)
    cp(full("icol"), full("i16"))
    ms(full("bm"), 0.0)
    add("V", 84, lambda g, T, e: g.vector.tensor_copy(T.bm[:, 15:128:16], T.z8[:, :]), [full("z8")], [full("bm")])
    for n, op, v in (("m12", A.is_lt, 12.0), ("c12", A.is_equal, 12.0), ("c13", A.is_equal, 13.0), ("c14", A.is_equal, 14.0),
                     ("ge13", A.is_ge, 13.0), ("ge14", A.is_ge, 14.0)):
        ts(full(n), full("icol"), v, op)
    cp(full("wtf"), full("wts"))
    for k in range(3):
        sm(full("WR%d" % k), full("bm"), full("c1%d" % (2 + k)))
    sm(full("WX"), full("bm"), ("wtf", 0, 1))
    sm(full("WY"), full("bm"), ("wtf", 1, 2))
    cp(full("ident"), ("idw", 2, 130))
    ts(full("nident"), ("idw", 2, 130), -1.0, A.mult)
    ts(full("thv"), full("mrow"), full("icol"), A.is_gt, full("m12"), A.mult)
    ts(full("ths"), full("thv"), 256.0, A.mult, -256.0, A.add)
    sa(full("sil"), full("icol"), F.Silu, scale=-SL, bias=-SL)
    ts(full("wc"), full("sil"), -1.5 * BIG, A.mult, full("m12"), A.mult)
    sm(full("WE"), full("bm"), full("wc"))
    ts(full("tha"), full("mrow"), 3.0, A.add, full("icol"), A.is_gt)
    ts(full("thb"), full("mrow"), 0.0, A.is_gt, full("m12"), A.mult)
    tt(full("th3"), full("tha"), full("thb"), A.mult)

    def edit_constants():
        gi(full("trow"), [[0, 2], [1, 128]], 0, 0, True)
        gi(full("t16a"), [[0, 2], [16, 8]], 0, 0, True)
        gi(full("iot"), [[256, 8208]], 0, 0, True)
        ts(full("t16"), full("t16a"), full("icol"), A.add)
        ts(full("dump16"), full("t16"), 8192.0, A.add)
        sm(full("isym"), ("idw", 2, 130), full("m12"))
        sm(full("sh1"), ("idw", 3, 131), full("ge13"))
        sm(full("sh2"), ("idw", 4, 132), full("ge14"))
        ts(full("sel1"), ("mrow", 0, 16), 2.0, A.is_equal)
        ts(full("sel2"), ("mrow", 0, 16), 1.0, A.is_equal)
        sm(full("mt"), ("mrow", 0, 16), full("c12"))
        ts(full("mid"), full("icol"), 15.0, A.is_lt)
        tt(full("wcm"), full("mid"), full("m12"), A.subtract)
        sm(full("spa"), ("idw", 1, 129), full("wcm"))
        tt(full("spl"), full("spa"), full("isym"), A.add)

    def under(rd, c, st, q):
        ml = c_("ml", c)
        if (rd, c, st) in Z_V:
            tt(c_("zz", c), full("thv"), c_(q, c), A.mult, ind=ml)
            return
        for h in (0, 512):
            sa(c_("rr", c, h, h + 512), full("ths"), F.Copy, ind=c_("ml", c, h // 16, h // 16 + 32))
            mm(("pw%d" % c, 0, 512), (full("ident"), c_(q, c, h, h + 512)), (full("ident"), c_("rr", c, h, h + 512)))
            sa(c_("zz", c, h, h + 512), ("pw%d" % c, 0, 512), F.Relu)

    def diff(c, out, mk, q, ind, byS):
        if not byS:
            tt(out, mk, c_(q, c), A.subtract, ind=ind)
            return
        for h in (0, 512):
            sa(c_("rr", c, h, h + 512), mk, F.Copy, ind=(ind[0], ind[1] + h // 16, ind[1] + h // 16 + 32))
            mm(("pw%d" % c, 0, 512), (full("ident"), c_("rr", c, h, h + 512)), (full("nident"), c_(q, c, h, h + 512)))
            sa((out[0], out[1] + h, out[1] + h + 512), ("pw%d" % c, 0, 512), F.Copy)

    def search(rd, c):
        q = "qa" if rd == 0 else "qb"
        mk = ("mk0" if rd == 0 else "mk1", 0, W)
        pn, pw = "pn%d" % c, "pw%d" % c
        u2, R0, R1, ky = (pn, 64, 128), (pn, 128, 192), (pn, 192, 256), (pn, 448, 512)
        tA, tB = ("vp", c * 128, c * 128 + 64), ("vp", c * 128 + 64, c * 128 + 128)
        hit = c_("hit", c)
        rq = lambda k: c_("rq", c, NN * k, NN * k + NN)
        cur[0] = "%d%d0" % (rd, c)
        pas((pn, 256, 320), "WR0", c_(q, c))
        cp(c_("ml", c), (pn, 256, 320))
        sa(rq(0), (pn, 256, 320), F.Copy)
        for st in range(S):
            cur[0] = "%d%d%d" % (rd, c, st)
            m = rq(0) if st == 0 else c_("m%d" % (st + 1), c)
            under(rd, c, st, q)
            sa(c_("w97", c), m, F.Identity, scale=97.0)
            sa(ky, m, F.Identity, scale=8192.0, bias=float((st + 1) << 17))
            sa(c_("thr0", c), m, F.Silu, scale=-SL)
            sa(c_("thr", c), c_("thr0", c), F.Abs, scale=BIG)
            pas((pn, 0, 64), "WX", c_("zz", c))
            pas(u2, "WY", c_("zz", c))
            cp(c_("ui", c), (pn, 0, 128))
            ts(c_("ac", c), c_("ui", c), 4095, A.bitwise_and)
            tt(tA, u2, c_("w97", c), A.add)
            tt(c_("pp", c), c_("ac", c, 0, NN), c_("ac", c, NN, 2 * NN), A.mult)
            ts(c_("kk", c), c_("pp", c), 5, A.arith_shift_right)
            tt(c_("ss", c), tA, c_("kk", c), A.add)
            ts(c_("hi", c), c_("ss", c), W - 1, A.bitwise_and)
            cp(c_("hl", c), c_("hi", c))
            tt(ky, ky, c_("hi", c), A.add)
            if rd == 0 and c == 0:
                x8 = ("act", 8 * st, 8 * st + 8)
                ts(x8, (m[0], m[1], m[1] + 8), 0.0, A.is_gt)
                tt(("ka", 8 * st, 8 * st + 8), (pn, 448, 456), x8, A.mult)
            diff(c, c_("dd", c), mk, q, c_("hl", c), (rd, c, st) in D_S)
            if st == 0:
                for k in (1, 2):
                    pas((pn, 256 + 64 * k, 320 + 64 * k), "WR%d" % k, c_(q, c))
                sa(c_("rq", c, NN, 3 * NN), (pn, 320, 448), F.Copy)
                tt(c_("xx", c), (pn, 256, 384), c_("rq", c, NN, 3 * NN), A.subtract)
            pas((pw, 0, 64), "WE", c_("dd", c))
            if st < 2:
                pas(R0, "WR0", c_("dd", c))
            if st < 1:
                pas(R1, "WR1", c_("dd", c))
            sa((pw, 64, 128), (pw, 0, 64), F.Abs)
            tt(hit, (pw, 64, 128), c_("thr", c), A.is_lt)
            if st < 2:
                nx = c_("m%d" % (st + 2), c)
                if st == 0:
                    x, old = c_("xx", c, 0, NN), rq(1)
                else:
                    x, old = c_("x2", c), c_("n2", c)
                    tt(x, rq(0), old, A.subtract)
                tt(tB, R0, x, A.add)
                tt(tB, tB, hit, A.mult)
                tt(nx, tB, old, A.add)
                cp(c_("ml", c), nx)
            if st == 0:
                tt(c_("kb", c), ky, hit, A.mult)
                tt(tA, R1, c_("xx", c, NN, 2 * NN), A.add)
                tt(tA, tA, hit, A.mult)
                tt(c_("n2", c), tA, rq(2), A.add)
            else:
                tt(tA, ky, hit, A.mult)
                tt(c_("kb", c), tA, c_("kb", c), A.max)

    def learn(rd, c):
        q = "qa" if rd == 0 else "qb"
        nw = "nwa" if rd == 0 else "nwb"
        mk = ("mk0" if rd == 0 else "mk1", 0, W)
        cur[0] = "%d%d3" % (rd, c)
        cp(c_("ki", c), c_("kb", c))
        ts(c_("bi", c), c_("ki", c), W - 1, A.bitwise_and)
        cp(c_("bl", c), c_("bi", c))
        diff(c, c_("ld", c), mk, q, c_("bl", c), (rd, c) in L_S)
        ts(c_("mbi", c), c_("ki", c), 13, A.arith_shift_right)
        cp(c_("mbl", c), c_("mbi", c))
        for h in (0, 512):
            tt(c_("lm", c, h, h + 512), full("th3"), c_("ld", c, h, h + 512), A.mult, ind=c_("mbl", c, h // 16, h // 16 + 32))
            mm(("pw%d" % c, 0, 512), (full("ident"), c_(q, c, h, h + 512)), (full("ident"), c_("lm", c, h, h + 512)))
            sa(c_(nw, c, h, h + 512), ("pw%d" % c, 0, 512), F.Copy)

    def move(c):
        def f(g, T, e):
            core, rank, topo = e
            moves, k = [], 0
            for d in range(1, 8):
                s = (rank + d) % 8
                dst = T.cores[s]
                en = topo.engines(core, dst)
                if topo.chip(dst) == topo.chip(core):
                    eng = en[-1]
                else:
                    eng = (en[0::2] + en[1::2])[k]
                    k += 1
                ad = topo.addr(dst)
                moves.append(RemoteDMATransfer(
                    dst_ids=[DstId(rid=ad[0], pnc=ad[1])], dma_engine_mask=1 << eng, remote_sem=T.sem["arr%d" % c],
                    src=T.nwa[:, c * CH + 128 * s:c * CH + 128 * s + 128],
                    dst=T.qb[:, c * CH + 128 * rank:c * CH + 128 * rank + 128]))
            return g.remote_dma_fused(moves, local_sem=T.sem["snt%d" % c])
        i = add("G", 1500, f, [c_("nwa", c)], [], sem="none%d" % c, inc=0)
        add("arr%d" % c, 0, None, [], [c_("qb", c)], sem="arr%d" % c, inc=7, lat=7000, deps=(i,))

        def f2(g, T, e):
            a = c * CH + 128 * e[1]
            return g.sync.dma_start(T.qb[:, a:a + 128], T.nwa[:, a:a + 128])
        k = add("Y", 60, f2, [c_("nwa", c)], [], sem="slf%d" % c, inc=16, lat=2500)
        acc["qb"].append((k, "Y", c * CH, c * CH + CH, True))

    def edits():
        e8 = lambda n: c_(n, 0, 0, 8)
        a8 = lambda n, k: (n, 8 * k, 8 * k + 8)
        tt(full("kam"), a8("ka", 0), a8("ka", 1), A.max)
        tt(full("kam"), full("kam"), a8("ka", 2), A.max)
        cp(full("kai"), full("kam"))
        ts(full("fi"), full("kai"), W - 1, A.bitwise_and)
        ts(full("mfi"), full("kai"), 13, A.arith_shift_right, 15, A.bitwise_and)
        ts(full("sbi"), e8("ki"), 17, A.arith_shift_right)
        cp(full("sbl"), full("sbi"))
        cp(full("mfl"), full("mfi"))
        tt(full("ed1"), full("kam"), e8("kb"), A.is_gt)
        ts(full("ed0"), e8("kb"), 0.0, A.is_gt)
        for k in (0, 1):
            tt(a8("ed", k), full("ed1"), full("ed0"), A.mult)
        ts(a8("fbm", 0), full("fi"), -8192.0, A.add)
        ts(a8("fbm", 1), e8("bi"), -8192.0, A.add)
        tt(full("fbe"), full("fbm"), full("ed"), A.mult)
        ts(full("flu"), full("fbe"), 8192.0, A.add)
        ts(full("nb"), full("fbe"), -256.0, A.mult, -2097152.0, A.add)
        tt(full("krow"), full("iot"), full("trow"), A.add, ind=full("flu"))
        for k in range(16):
            h, n = 128 * (k // 8), 16 * (k % 8 + 1)
            sa(("dk", 128 * k, 128 * k + n), ("krow", h, h + n), F.Identity, bias=("nb", k, k + 1))
            add("V", vdur(n), lambda g, T, e, k=k, n=n: g.vector.tensor_reduce(
                T.first[:, k:k + 1], T.dk[:, 128 * k:128 * k + n], AxisListType.X, A.min, apply_absolute_value=True),
                [("dk", 128 * k, 128 * k + n)], [("first", k, k + 1)])
        tt(full("win"), full("first"), full("t16"), A.is_equal)
        tt(full("win"), full("win"), full("ed"), A.mult)
        tt(full("gg"), full("fbm"), full("t16"), A.subtract)
        tt(full("gg"), full("gg"), full("win"), A.mult)
        tt(full("tgt"), full("gg"), full("dump16"), A.add)
        cp(full("tgu"), full("tgt"))
        sa(full("g0"), ("mk0", 0, W), F.Copy, ind=e8("bl"))
        tt(full("ga1"), full("sel1"), full("g0"), A.mult, ind=full("sbl"))
        tt(full("ga2"), full("sel2"), full("g0"), A.mult, ind=full("sbl"))
        mm(("pe", 0, 128), (full("sh1"), full("ga1")), (full("sh2"), full("ga2")), (full("isym"), ("qa", 0, 128)))
        sa(full("wnew"), ("pe", 0, 128), F.Copy)
        scat(full("mk1"), ("tgu", 0, 8), full("wnew"))
        sa(full("g1"), ("mk1", 0, W), F.Copy, ind=e8("bl"))
        sa(full("mfw"), full("mt"), F.Copy, ind=full("mfl"))
        mm(("pe", 0, 128), (full("spl"), full("g1")), (full("ident"), full("mfw")))
        sa(full("snew"), ("pe", 0, 128), F.Copy)
        scat(full("mk1"), ("tgu", 8, 16), full("snew"))

    def blocks(c):
        ts(c_("ybx", c), c_("kb", c), 0.0, A.is_equal, -1.0, A.mult)
        add("V", vdur(64, 2), lambda g, T, e: g.vector.tensor_tensor(T.yby[:, :, 8 * c:8 * c + 8], ap(T, c_("ybx", c)),
            ap(T, c_("bi", c)), A.add), [c_("ybx", c), c_("bi", c)], [("yby", 64 * c, 64 * c + 64)])
        if c == NC - 1:
            add("Y", 60, lambda g, T, e: g.sync.dma_start(T.yb[:, :], T.yby[:, :, :]),
                [("yby", 0, 192)], [], sem="lyb", inc=16, lat=2500)

    def store(c):
        for s in range(8):
            q = "S" if c == NC - 1 and s >= 6 else "Y"
            a = c * CH + 128 * s

            def f(g, T, e, a=a, s=s, q=q):
                return (g.sync if q == "Y" else g.scalar).dma_start(
                    T.yq[:, 384 * s + 128 * c:384 * s + 128 * c + 128], T.nwb[:, a:a + 128])
            add(q, 60, f, [("nwb", a, a + 128)], [], sem="out%d" % c, inc=16, lat=2500)

    for c in range(NC):
        search(0, c)
        learn(0, c)
        move(c)
    cur[0] = "k"
    edit_constants()
    cur[0] = "e"
    edits()
    for c in range(NC):
        search(1, c)
        learn(1, c)
        blocks(c)
        store(c)
    return ops


QSEM = {"T": "sT", "V": "sV", "S": "sS", "G": "sG"}


def schedule(ops):
    n = len(ops)
    kids = [[] for _ in range(n)]
    need = [len(o["deps"]) for o in ops]
    for i, o in enumerate(ops):
        for d in o["deps"]:
            kids[d].append(i)
    tail = [0.0] * n
    for i in range(n - 1, -1, -1):
        tail[i] = ops[i]["dur"] + ops[i]["lat"] + max([tail[k] + WAKE for k in kids[i]] or [0.0])
    free, ready, est, done = {}, {}, [0.0] * n, [0.0] * n
    for i in range(n):
        ready.setdefault(ops[i]["q"], [])
        free[ops[i]["q"]] = 0.0
        if need[i] == 0:
            ready[ops[i]["q"]].append(i)
    order = []
    for _ in range(n):
        best = None
        for q, lst in ready.items():
            if lst:
                t = max(free[q], min(est[i] for i in lst))
                if best is None or t < best[0]:
                    best = (t, q)
        t, q = best
        i = max((i for i in ready[q] if est[i] <= t), key=lambda i: (tail[i] + ops[i]["pr"] + BIAS.get(ops[i]["tag"], 0.0), -i))
        ready[q].remove(i)
        free[q] = t + ops[i]["dur"]
        done[i] = free[q] + ops[i]["lat"]
        order.append(i)
        for k in kids[i]:
            est[k] = max(est[k], done[i] + WAKE)
            need[k] -= 1
            if need[k] == 0:
                ready[ops[k]["q"]].append(k)
    return order, max(done), done


PLAN = {}


def rank_program(g, core, T, topo):
    rank = T.rank_of(core)
    if rank is None:
        return
    if not PLAN:
        PLAN["ops"] = graph()
        PLAN["order"] = schedule(PLAN["ops"])[0]
    ops, order = PLAN["ops"], PLAN["order"]
    env = (core, rank, topo)
    eng = {"T": g.tensor, "V": g.vector, "S": g.scalar, "G": g, "Y": g.sync}
    total = {}
    for o in ops:
        if o["sem"] and o["inc"]:
            total[o["sem"]] = total.get(o["sem"], 0) + o["inc"]
    count, stamp, clock, known = {}, {}, {}, {}
    for i in order:
        o = ops[i]
        q = o["q"]
        kn = known.setdefault(q, {})
        want = {}
        for d in o["deps"]:
            s, v = stamp[d]
            if kn.get(s, 0) < v:
                want[s] = max(want.get(s, 0), v)
        for s in sorted(want, key=lambda s: -len(clock[(s, want[s])])):
            v = want[s]
            if kn.get(s, 0) >= v:
                continue
            if o["fn"] is not None and not s.startswith("none"):
                eng[q].wait_ge(T.sem[s], v)
            kn[s] = max(kn.get(s, 0), v)
            for s2, v2 in clock[(s, v)].items():
                kn[s2] = max(kn.get(s2, 0), v2)
        ins = o["fn"](g, T, env) if o["fn"] is not None else None
        if o["sem"] is None:
            s = QSEM[q]
            count[s] = count.get(s, 0) + 1
            ins.then_inc(T.sem[s], 1)
            v = count[s]
            prev = clock.get((s, v - 1), {})
        else:
            s = o["sem"]
            v = total.get(s, 1)
            if ins is not None and o["inc"]:
                ins.then_inc(T.sem[s], o["inc"])
            prev = clock.get((s, v), {})
        stamp[i] = (s, v)
        ck = {}
        if not s.startswith("arr"):
            ck = dict(prev)
            for s2, v2 in kn.items():
                ck[s2] = max(ck.get(s2, 0), v2)
        clock[(s, v)] = ck
    for s in SEMAPHORES:
        if s in count:
            g.wait_ge(T.sem[s], count[s])
        else:
            g.wait_ge(T.sem[s], total[s] if s in total else 7)
